import numpy as np
import ml_dtypes


def mxq(x, axis, fmt="e4m3"):
    dtype, down = {"e4m3": (ml_dtypes.float8_e4m3fn, 7), "e5m2": (ml_dtypes.float8_e5m2, 14)}[fmt]
    v = np.moveaxis(np.asarray(x, np.float32).astype(ml_dtypes.bfloat16).astype(np.float64), axis, -1)
    blocks = v.reshape(v.shape[:-1] + (-1, 32))
    amax = np.abs(blocks).max(-1, keepdims=True)
    byte = np.maximum(np.where(amax > 0, np.frexp(amax)[1] - 1 + 127, 0) - down, 1)
    scale = np.exp2(byte - 127.0)
    codes = (blocks / scale).astype(np.float32).astype(dtype).astype(np.float64)
    return np.moveaxis((codes * scale).reshape(v.shape), -1, axis)


WIDE = False


def mx_kscale(k):
    if not WIDE:
        return np.ones(k)
    levels = np.array([10, -10, 5, -5, 0])
    if k % 512:
        return np.exp2(np.random.permutation(np.resize(levels, k // 32))).repeat(32)
    a = np.empty((k // 512, 16))
    for p in range(k // 512):
        a[p, :8] = np.random.permutation(np.resize(levels, 8))
        for g in range(8):
            far = levels[np.abs(levels - a[p, g]) >= 10]
            a[p, g + 8] = far[np.random.randint(len(far))]
    return np.exp2(a.ravel()).repeat(32)


def f64(x):
    return np.asarray(x).astype(np.float64)


def striped(idx):
    return np.tile(idx.reshape(-1, 16).T, (8, 1)).astype(np.uint16)


def unstriped(offs):
    return offs[:16].T.reshape(-1).astype(np.int64)


E2M1 = np.array([0.0, 0.5, 1.0, 1.5, 2.0, 3.0, 4.0, 6.0, -0.0, -0.5, -1.0, -1.5, -2.0, -3.0, -4.0, -6.0])


def pack_weight(w, fmt):
    k, n = w.shape
    w = f64(np.asarray(w, np.float32).astype(ml_dtypes.bfloat16)).reshape(k // 32, 32, n)
    amax = np.abs(w).max(1)
    if fmt == "e4m3":
        byte = np.frexp(amax)[1] - 1 + 127 - 7
    else:
        mant, ex = np.frexp(amax / 6.0)
        byte = np.where(mant > 0.5, ex, ex - 1) + 127
    byte = np.clip(np.where(amax > 0, byte, 1), 1, 254)
    scaled = (w * np.exp2(127.0 - byte)[:, None, :]).reshape(k, n).astype(np.float32)
    by_word = np.ascontiguousarray(scaled.reshape(k // 512, 128, 4, n).transpose(0, 1, 3, 2))
    if fmt == "e4m3":
        words = by_word.astype(ml_dtypes.float8_e4m3fn).view(np.uint8)
    else:
        c = by_word.astype(ml_dtypes.float4_e2m1fn).view(np.uint8) & 0xF
        words = (c[..., 0::2] | (c[..., 1::2] << 4)).reshape(k // 512, 128, 2 * n)
    return np.ascontiguousarray(words), np.ascontiguousarray(byte.astype(np.uint8).reshape(k // 512, 16, n))


def unpack_weight(words, scales, fmt):
    g, _, n = scales.shape
    words = np.ascontiguousarray(words).reshape(g, 128, n, -1)
    if fmt == "e4m3":
        vals = words.view(ml_dtypes.float8_e4m3fn).astype(np.float64)
    else:
        nib = np.empty((g, 128, n, 4), np.uint8)
        nib[..., 0::2] = words & 0xF
        nib[..., 1::2] = words >> 4
        vals = E2M1[nib]
    vals = vals * np.repeat(np.exp2(scales.astype(np.float64) - 127.0), 8, axis=1)[..., None]
    return vals.transpose(0, 1, 3, 2).reshape(g * 512, n)


def gelu(v):
    return 0.5 * v * (1.0 + np.tanh(np.sqrt(2.0 / np.pi) * (v + 0.044715 * v**3)))


K, K2, H, N, T, S, P, TO = 512, 1024, 1024, 512, 2048, 1024, 512, 2048

def setup_inputs():
    n = np.random.standard_normal
    s, s2, u = mx_kscale(K)[:, None], mx_kscale(K2)[:, None], mx_kscale(H)[:, None]
    perm = np.random.permutation(TO)
    d = {}
    d["tab_words"], d["tab_scales"] = pack_weight(n((K, T)) * s, "e4m3")
    d["tab2_words"], d["tab2_scales"] = pack_weight(n((K2, T)) * s2, "e4m3")
    d["offs"] = striped(np.random.permutation(T)[:S])
    d["offs2"] = striped(np.random.permutation(T)[:P])
    d["pos1"] = striped(np.random.permutation(S)[:P])
    d["offs3"] = striped(perm[:S])
    d["offs4"] = striped(perm[S:S + P])
    d["w1"] = (0.9 * n((K, H)) / np.sqrt(K) / s).astype(np.float32)
    d["w2_words"], d["w2_scales"] = pack_weight(0.5 * n((K, H)) / np.sqrt(K) / s, "e2m1")
    d["w3"] = (1.6 * n((K2, H)) / np.sqrt(K2) / s2).astype(np.float32)
    d["gain"] = (np.exp(0.3 * n(H)) * u[:, 0]).astype(np.float32)
    d["w4_words"], d["w4_scales"] = pack_weight(1.4 * n((H, N)) / np.sqrt(H) / u, "e2m1")
    d["w5"] = (0.6 * n((H, N)) / np.sqrt(H) / u).astype(np.float32)
    d["w6_words"], d["w6_scales"] = pack_weight(0.8 * n((K2, N)) / np.sqrt(K2) / s2, "e4m3")
    d["page1"] = n((N, TO)).astype(np.float32)
    d["wg1"] = np.exp(0.3 * n((128, S))).astype(np.float32)
    d["wg2"] = np.exp(0.3 * n((128, P))).astype(np.float32)
    return d

def reference(tab_words, tab_scales, tab2_words, tab2_scales, offs, offs2, pos1, offs3, offs4, w1, w2_words, w2_scales, w3, gain, w4_words, w4_scales, w5, w6_words, w6_scales, page1, wg1, wg2):
    v = unpack_weight(tab_words, tab_scales, "e4m3")[:, unstriped(offs)]
    v2 = unpack_weight(tab2_words, tab2_scales, "e4m3")[:, unstriped(offs2)]
    h1 = (mxq(f64(w1), 0, "e4m3").T @ v) + np.cos(unpack_weight(w2_words, w2_scales, "e2m1").T @ v)
    h2 = mxq(f64(w3), 0, "e4m3").T @ v2
    z = np.zeros((H, S + P))
    z[:, :S] = np.tanh(h1)
    z[:, S:] = np.maximum(h2, h1[:, unstriped(pos1)])
    zq = mxq(z * f64(gain)[:, None], 0, "e4m3")
    y1 = unpack_weight(w4_words, w4_scales, "e2m1").T @ zq[:, :S]
    y2 = mxq(f64(w5), 0, "e4m3").T @ zq[:, S:] + unpack_weight(w6_words, w6_scales, "e4m3").T @ v2
    out = f64(page1).copy()
    out[:, unstriped(offs3)] = np.tile(f64(wg1), (N // 128, 1)) * y1
    out[:, unstriped(offs4)] = np.tile(f64(wg2), (N // 128, 1)) * y2
    return out

@@ -1,0 +1,338 @@
+import math
+from contextlib import ExitStack
+
+import concourse.mybir as mybir
+
+K, K2, H, N, T, S, PB, TO = 512, 1024, 1024, 512, 2048, 1024, 512, 2048
+FLOPS = 2 * (2 * K * H * S + K2 * H * PB + H * N * S + H * N * PB + K2 * N * PB)
+
+F32 = mybir.dt.float32
+BF16 = mybir.dt.bfloat16
+I32 = mybir.dt.int32
+U32 = mybir.dt.uint32
+U16 = mybir.dt.uint16
+U8 = mybir.dt.uint8
+E4M3 = mybir.dt.float8_e4m3fn_x4
+E2M1 = mybir.dt.float4_e2m1fn_x4
+ALU = mybir.AluOpType
+ACT = mybir.ActivationFunctionType
+
+P = 128
+W = 512
+LCOLS = W // 16
+
+
+def tile_list_block_bid_features_kernel(
+    tc, tab_words, tab_scales, tab2_words, tab2_scales, offs, offs2, pos1, offs3, offs4,
+    w1, w2_words, w2_scales, w3, gain, w4_words, w4_scales, w5, w6_words, w6_scales,
+    page1, wg1, wg2, out,
+):
+    nc = tc.nc
+    with ExitStack() as ctx:
+        held = ctx.enter_context(tc.tile_pool(name="held", bufs=1))
+        ring = ctx.enter_context(tc.tile_pool(name="ring", bufs=2))
+        psum = ctx.enter_context(tc.psum_pool(name="psum", bufs=2))
+
+        def keep(name, shape, dtype):
+            return held.tile(shape, dtype, name=name, align_bytes=64)
+
+        def load_list(name, src):
+            lst = held.tile(list(src.shape), U16, name=name)
+            nc.sync.dma_start(lst[:], src)
+            return lst
+
+        def load(name, shape, dtype, src, tag=None):
+            dst = held.tile(shape, dtype, name=name, tag=tag or name, align_bytes=64)
+            nc.sync.dma_start(out=dst[:], in_=src)
+            return dst
+
+        def load_words(name, words, tag=None):
+            flat = words.rearrange("p c i -> p (c i)").bitcast(I32)
+            return load(name, list(flat.shape), I32, flat, tag)
+
+        def load_stacked_scales(name, scales, queue, zero):
+            passes, rows, width = scales.shape
+            plane = keep(name, [P, width], U8)
+            zero.memset(plane[:].bitcast(I32), 0)
+            for q in range(4):
+                queue.dma_start(
+                    out=plane[32 * q : 32 * q + 4 * passes, :].bitcast(I32),
+                    in_=scales[:, 4 * q : 4 * q + 4, :].bitcast(I32),
+                )
+            return plane
+
+        def load_repeated_scales(name, scales):
+            rows, width = scales.shape
+            plane = keep(name, [P, width], U8)
+            for q in range(4):
+                nc.sync.dma_start(
+                    out=plane[32 * q : 32 * (q + 1), :].bitcast(I32),
+                    in_=scales[4 * q : 4 * q + 4, :].bitcast(I32).partition_broadcast(8),
+                )
+            return plane
+
+        def load_raw(w, a, cols, tag):
+            rows = w[W * a : W * (a + 1), cols].rearrange("(p j) c -> p j c", j=4)
+            return load("raw", [P, 4, W], F32, rows, tag)
+
+        def copy_on(engine, dst, src):
+            if engine == "scalar":
+                nc.scalar.copy(out=dst, in_=src)
+            else:
+                nc.vector.tensor_copy(out=dst, in_=src)
+
+        def quantise(grouped, codes, scales):
+            nc.vector.quantize_mx(out=codes[:].bitcast(E4M3), scales=scales[:], in_=grouped[:])
+
+        def round_dealt(raw, engine):
+            grouped = ring.tile([P, 4 * W], BF16, name="w_grouped", bufs=2, align_bytes=64)
+            copy_on(
+                engine,
+                grouped[:].rearrange("p (t m j) -> p m j t", t=4, j=4),
+                raw[:].rearrange("p j (m t) -> p m j t", t=4),
+            )
+            return grouped
+
+        def interleave(rows, engine, name):
+            grouped = ring.tile([P, 4 * W], BF16, name=name, bufs=2, align_bytes=64)
+            copy_on(
+                engine,
+                grouped[:].rearrange("p (c i j) -> p c j i", i=4, j=4),
+                rows[:].rearrange("p j (c i) -> p c j i", i=4),
+            )
+            return grouped
+
+        def quantised_weight(name, grouped):
+            codes = keep(name + "_codes", [P, W], U32)
+            scales = keep(name + "_scales", [P, W], U8)
+            quantise(grouped, codes, scales)
+            return codes, scales
+
+        idx = load_list("idx", offs)
+        w2_w = load("w2_w", [P, H // 2], I32, w2_words[0].bitcast(I32))
+        w2_s = load_repeated_scales("w2_s", w2_scales[0])
+        tab_w = load_words("tab_w", tab_words[0], "slab0")
+        tab_s = load_repeated_scales("tab_s", tab_scales[0])
+        w1_raw = [load_raw(w1, 0, slice(W * b, W * (b + 1)), "slab%d" % (1 + b)) for b in range(2)]
+        gain_sb = load("gain_sb", [P, 2, 4], F32, gain.rearrange("(b p t) -> p b t", b=2, t=4))
+        idx2 = load_list("idx2", offs2)
+        tab2_w = [load_words("tab2_w%d" % a, tab2_words[a], "slab%d" % a) for a in range(2)]
+        tab2_s = load_stacked_scales("tab2_s", tab2_scales, nc.gpsimd, nc.gpsimd)
+        w4_w = [load("w4_w%d" % a, [P, N // 2], I32, w4_words[a].bitcast(I32)) for a in range(2)]
+        w4_s = keep("w4_s", [P, 2, N], U8)
+        nc.gpsimd.memset(w4_s[:].bitcast(I32), 0)
+        for q in range(4):
+            nc.gpsimd.dma_start(
+                out=w4_s[32 * q : 32 * q + 4, :, :].bitcast(I32),
+                in_=w4_scales[:, 4 * q : 4 * q + 4, :].rearrange("a r n -> r a n").bitcast(I32),
+            )
+        w6_s = load_stacked_scales("w6_s", w6_scales, nc.gpsimd, nc.gpsimd)
+        idx3 = load_list("idx3", offs3)
+        wg1_sb = load("wg1_sb", [P, S], F32, wg1)
+        pages = [load("page%d" % i, [P, TO], F32, page1[P * i : P * (i + 1), :], "slab%d" % i) for i in range(4)]
+        peak = load_list("peak", pos1)
+        idx4 = load_list("idx4", offs4)
+        wg2_sb = load("wg2_sb", [P, PB], F32, wg2)
+        w6_w = [load_words("w6_w%d" % a, w6_words[a]) for a in range(2)]
+
+        v_w, v_s = [], []
+
+        def gather_v(c):
+            part = idx[:, LCOLS * c : LCOLS * (c + 1)]
+            words = keep("v_w%d" % c, [P, W], U32)
+            scales = keep("v_s%d" % c, [P, W], U8)
+            nc.vector.tensor_copy(words[:], tab_w[:].bitcast(U32).indirect(part))
+            nc.vector.tensor_copy(scales[:], tab_s[:].indirect(part))
+            v_w.append(words)
+            v_s.append(scales)
+
+        w2d_w = keep("w2d_w", [P, 2 * H], U8)
+        w2d_s = keep("w2d_s", [P, H], U8)
+        nc.vector.tensor_copy(
+            out=w2d_w[:].bitcast(U16).rearrange("p (b t m) -> p b m t", b=2, t=4),
+            in_=w2_w[:].bitcast(U16).rearrange("p (b m t) -> p b m t", b=2, t=4),
+        )
+        nc.vector.tensor_copy(
+            out=w2d_s[:].rearrange("p (b t m) -> p b m t", b=2, t=4),
+            in_=w2_s[:].rearrange("p (b m t) -> p b m t", b=2, t=4),
+        )
+        gather_v(0)
+        w1_q = [
+            quantised_weight("w1_%d" % b, round_dealt(w1_raw[b], "vector" if b == 0 else "scalar"))
+            for b in range(2)
+        ]
+        gather_v(1)
+
+        h1 = [keep("h1_%d" % b, [P, 4, S], F32) for b in range(2)]
+
+        def cosine_of(step, whole_on):
+            c, b, pair = step // 4, step // 2 % 2, step % 2
+            turns = ring.tile([P, 2, W], F32, name="turns", bufs=4)
+            for e in range(2):
+                col0 = W * b + P * (2 * pair + e)
+                x = psum.tile([P, W], F32, name="x", bufs=2)
+                nc.tensor.matmul_mx(
+                    out=x[:],
+                    lhsT=w2d_w[:, 2 * col0 : 2 * (col0 + P)].bitcast(E2M1),
+                    lhsT_scale=w2d_s[:, col0 : col0 + P],
+                    rhs=v_w[c][:].bitcast(E4M3),
+                    rhs_scale=v_s[c][:],
+                    start=True,
+                    stop=True,
+                )
+                nc.scalar.activation(turns[:, e, :], x[:], ACT.Abs, scale=1.0 / (2.0 * math.pi))
+            if whole_on == "scalar":
+                whole = ring.tile([P, 2, W], U32, name="whole", bufs=2)
+                nc.scalar.activation(whole[:], turns[:], ACT.Identity, bias=0.25)
+                whole_int = whole[:].bitcast(I32)
+            else:
+                whole = ring.tile([P, 2, W], I32, name="whole", bufs=2)
+                nc.vector.tensor_scalar(whole[:], turns[:], 0.25, None, ALU.add)
+                whole_int = whole[:]
+            nc.vector.tensor_tensor(turns[:], turns[:], whole_int, ALU.subtract)
+            nc.scalar.activation(turns[:], turns[:], ACT.Sin, scale=2.0 * math.pi, bias=0.5 * math.pi)
+            return turns
+
+        def h1_of(step, cosine):
+            c, b, pair = step // 4, step // 2 % 2, step % 2
+            for e in range(2):
+                t = 2 * pair + e
+                acc = psum.tile([P, W], F32, name="acc", bufs=3)
+                nc.tensor.matmul_mx(
+                    out=acc[:],
+                    lhsT=w1_q[b][0][:, P * t : P * (t + 1)].bitcast(E4M3),
+                    lhsT_scale=w1_q[b][1][:, P * t : P * (t + 1)],
+                    rhs=v_w[c][:].bitcast(E4M3),
+                    rhs_scale=v_s[c][:],
+                    start=True,
+                    stop=True,
+                )
+                nc.vector.tensor_tensor(h1[b][:, t, W * c : W * (c + 1)], acc[:], cosine[:, e, :], ALU.add)
+
+        def quantised_z(pre, b, gain_on, weave_on):
+            rounded = ring.tile([P, 4, W], BF16, name="rounded", bufs=2)
+            for t in range(4):
+                factor = gain_sb[:, b, t : t + 1]
+                if gain_on == "scalar":
+                    nc.scalar.activation(rounded[:, t, :], pre[:, t, :], ACT.Copy, scale=factor)
+                else:
+                    nc.vector.tensor_scalar(rounded[:, t, :], pre[:, t, :], factor, None, ALU.mult)
+            grouped = interleave(rounded, weave_on, "z_grouped")
+            codes = ring.tile([P, W], U32, name="z_codes", bufs=4, align_bytes=64)
+            scales = ring.tile([P, W], U8, name="z_scales", bufs=4, align_bytes=64)
+            quantise(grouped, codes, scales)
+            return codes, scales
+
+        def z1_of(c, b, gain_on, weave_on):
+            pre = ring.tile([P, 4, W], F32, name="pre", bufs=2)
+            nc.scalar.activation(pre[:], h1[b][:, :, W * c : W * (c + 1)], ACT.Tanh)
+            return quantised_z(pre, b, gain_on, weave_on)
+
+        def product(passes):
+            y = psum.tile([P, W], F32, name="y", bufs=3)
+            for n, (lw, ls, rw, rs) in enumerate(passes):
+                nc.tensor.matmul_mx(
+                    out=y[:], lhsT=lw, lhsT_scale=ls, rhs=rw, rhs_scale=rs,
+                    start=(n == 0), stop=(n == len(passes) - 1),
+                )
+            y_sb = ring.tile([P, W], F32, name="y_sb", bufs=4)
+            nc.scalar.copy(out=y_sb[:], in_=y[:])
+            return y_sb
+
+        def y1_of(z, i):
+            return product([
+                (
+                    w4_w[a][:].bitcast(U8)[:, 2 * P * i : 2 * P * (i + 1)].bitcast(E2M1),
+                    w4_s[:, a, P * i : P * (i + 1)],
+                    z[a][0][:].bitcast(E4M3),
+                    z[a][1][:],
+                )
+                for a in range(2)
+            ])
+
+        def place_y1(y_sb, c, i):
+            nc.vector.tensor_tensor(
+                pages[i][:].indirect(idx3[:, LCOLS * c : LCOLS * (c + 1)]),
+                y_sb[:], wg1_sb[:, W * c : W * (c + 1)], ALU.mult,
+            )
+
+        z_first = []
+        cosines = {0: cosine_of(0, "vector")}
+        for step in range(8):
+            if step + 1 < 8:
+                cosines[step + 1] = cosine_of(step + 1, "vector" if step + 1 < 4 else "scalar")
+            if step in (5, 6):
+                z_first.append(z1_of(0, len(z_first), "vector", "vector"))
+            h1_of(step, cosines[step])
+
+        v2_w = []
+        for a in range(2):
+            words = keep("v2_w%d" % a, [P, PB], U32)
+            nc.vector.tensor_copy(words[:], tab2_w[a][:].bitcast(U32).indirect(idx2[:]))
+            v2_w.append(words)
+        v2_s = keep("v2_s", [P, PB], U8)
+        nc.vector.tensor_copy(v2_s[:], tab2_s[:].indirect(idx2[:]))
+
+        peaks = []
+        for b in range(2):
+            pre = ring.tile([P, 4, W], F32, name="peaks", bufs=2)
+            for t in range(4):
+                nc.vector.tensor_copy(pre[:, t, :], h1[b][:, t, :].indirect(peak[:]))
+            peaks.append(pre)
+
+        for i in range(4):
+            place_y1(y1_of(z_first, i), 0, i)
+
+        for b in range(2):
+            w3_q = [
+                quantised_weight(
+                    "w3_%d_%d" % (a, b),
+                    round_dealt(load_raw(w3, a, slice(W * b, W * (b + 1)), "slab%d" % (4 + a)), "scalar"),
+                )
+                for a in range(2)
+            ]
+            for t in range(4):
+                acc = psum.tile([P, W], F32, name="acc", bufs=3)
+                for a in range(2):
+                    nc.tensor.matmul_mx(
+                        out=acc[:],
+                        lhsT=w3_q[a][0][:, P * t : P * (t + 1)].bitcast(E4M3),
+                        lhsT_scale=w3_q[a][1][:, P * t : P * (t + 1)],
+                        rhs=v2_w[a][:].bitcast(E4M3),
+                        rhs_scale=v2_s[4 * a : P, :],
+                        start=(a == 0),
+                        stop=(a == 1),
+                    )
+                nc.vector.tensor_tensor(peaks[b][:, t, :], acc[:], peaks[b][:, t, :], ALU.max)
+
+        z_second = [z1_of(1, b, "scalar", "scalar") for b in range(2)]
+        w5_q = [
+            quantised_weight(
+                "w5_%d" % a,
+                interleave(load_raw(w5, a, slice(0, N), "slab%d" % (4 + a)), "scalar", "w_grouped"),
+            )
+            for a in range(2)
+        ]
+
+        z_third = []
+        for i in range(4):
+            place_y1(y1_of(z_second, i), 1, i)
+            if i in (0, 1):
+                b = len(z_third)
+                z_third.append(quantised_z(peaks[b], b, "scalar", "scalar"))
+        for i in range(4):
+            cols = slice(P * i, P * (i + 1))
+            y_sb = product(
+                [
+                    (w6_w[a][:, cols].bitcast(E4M3), w6_s[4 * a : P, cols],
+                     v2_w[a][:].bitcast(E4M3), v2_s[4 * a : P, :])
+                    for a in range(2)
+                ]
+                + [
+                    (w5_q[a][0][:, cols].bitcast(E4M3), w5_q[a][1][:, cols],
+                     z_third[a][0][:].bitcast(E4M3), z_third[a][1][:])
+                    for a in range(2)
+                ]
+            )
+            nc.vector.tensor_tensor(pages[i][:].indirect(idx4[:]), y_sb[:], wg2_sb[:], ALU.mult)
+            nc.sync.dma_start(out=out[P * i : P * (i + 1), :], in_=pages[i][:])

@@ -85,7 +85,7 @@ def tile_list_block_bid_features_kernel(
             nc.vector.quantize_mx(out=codes[:].bitcast(E4M3), scales=scales[:], in_=grouped[:])
 
         def round_dealt(raw, engine):
-            grouped = ring.tile([P, 4 * W], BF16, name="w_grouped", bufs=2, align_bytes=64)
+            grouped = ring.tile([P, 4 * W], BF16, name="w_grouped", bufs=3, align_bytes=64)
             copy_on(
                 engine,
                 grouped[:].rearrange("p (t m j) -> p m j t", t=4, j=4),
@@ -93,12 +93,12 @@ def tile_list_block_bid_features_kernel(
             )
             return grouped
 
-        def interleave(rows, engine, name):
-            grouped = ring.tile([P, 4 * W], BF16, name=name, bufs=2, align_bytes=64)
+        def interleave(rows, engine, name, bufs=2):
+            grouped = ring.tile([P, 4 * rows.shape[2]], BF16, name=name, bufs=bufs, align_bytes=64)
             copy_on(
                 engine,
                 grouped[:].rearrange("p (c i j) -> p c j i", i=4, j=4),
-                rows[:].rearrange("p j (c i) -> p c j i", i=4),
+                rows.rearrange("p j (c i) -> p c j i", i=4),
             )
             return grouped
 
@@ -108,11 +108,15 @@ def tile_list_block_bid_features_kernel(
             quantise(grouped, codes, scales)
             return codes, scales
 
+        warm = keep("warm", [P, 1], F32)
+        nc.vector.memset(warm[:], 0.0)
+        nc.scalar.activation(warm[:], warm[:], ACT.Silu)
+
         idx = load_list("idx", offs)
-        w2_w = load("w2_w", [P, H // 2], I32, w2_words[0].bitcast(I32))
-        w2_s = load_repeated_scales("w2_s", w2_scales[0])
-        tab_w = load_words("tab_w", tab_words[0], "slab0")
         tab_s = load_repeated_scales("tab_s", tab_scales[0])
+        w2_w = load("w2_w", [P, H // 2], I32, w2_words[0].bitcast(I32))
+        tab_w = load_words("tab_w", tab_words[0], "slab0")
+        w2_s = load_repeated_scales("w2_s", w2_scales[0])
         w1_raw = [load_raw(w1, 0, slice(W * b, W * (b + 1)), "slab%d" % (1 + b)) for b in range(2)]
         gain_sb = load("gain_sb", [P, 2, 4], F32, gain.rearrange("(b p t) -> p b t", b=2, t=4))
         idx2 = load_list("idx2", offs2)
@@ -139,7 +143,7 @@ def tile_list_block_bid_features_kernel(
 
         def gather_v(c):
             part = idx[:, LCOLS * c : LCOLS * (c + 1)]
-            words = keep("v_w%d" % c, [P, W], U32)
+            words = held.tile([P, W], U32, name="v_w%d" % c, tag="v_w0" if c == 0 else "w2_s", align_bytes=64)
             scales = keep("v_s%d" % c, [P, W], U8)
             nc.vector.tensor_copy(words[:], tab_w[:].bitcast(U32).indirect(part))
             nc.vector.tensor_copy(scales[:], tab_s[:].indirect(part))
@@ -210,32 +214,34 @@ def tile_list_block_bid_features_kernel(
                 nc.vector.tensor_tensor(h1[b][:, t, W * c : W * (c + 1)], acc[:], cosine[:, e, :], ALU.add)
 
         def quantised_z(pre, b, gain_on, weave_on):
-            rounded = ring.tile([P, 4, W], BF16, name="rounded", bufs=2)
+            width = pre.shape[2]
+            rounded = ring.tile([P, 4, width], BF16, name="rounded", bufs=2)
             for t in range(4):
                 factor = gain_sb[:, b, t : t + 1]
                 if gain_on == "scalar":
                     nc.scalar.activation(rounded[:, t, :], pre[:, t, :], ACT.Copy, scale=factor)
                 else:
                     nc.vector.tensor_scalar(rounded[:, t, :], pre[:, t, :], factor, None, ALU.mult)
-            grouped = interleave(rounded, weave_on, "z_grouped")
-            codes = ring.tile([P, W], U32, name="z_codes", bufs=4, align_bytes=64)
-            scales = ring.tile([P, W], U8, name="z_scales", bufs=4, align_bytes=64)
+            grouped = interleave(rounded[:], weave_on, "z_grouped")
+            codes = ring.tile([P, width], U32, name="z_codes", bufs=4, align_bytes=64)
+            scales = ring.tile([P, width], U8, name="z_scales", bufs=4, align_bytes=64)
             quantise(grouped, codes, scales)
             return codes, scales
 
         def z1_of(c, b, gain_on, weave_on):
             pre = ring.tile([P, 4, W], F32, name="pre", bufs=2)
             nc.scalar.activation(pre[:], h1[b][:, :, W * c : W * (c + 1)], ACT.Tanh)
-            return quantised_z(pre, b, gain_on, weave_on)
+            return quantised_z(pre[:], b, gain_on, weave_on)
 
         def product(passes):
-            y = psum.tile([P, W], F32, name="y", bufs=3)
+            width = passes[0][2].shape[1]
+            y = psum.tile([P, width], F32, name="y", bufs=3)
             for n, (lw, ls, rw, rs) in enumerate(passes):
                 nc.tensor.matmul_mx(
                     out=y[:], lhsT=lw, lhsT_scale=ls, rhs=rw, rhs_scale=rs,
                     start=(n == 0), stop=(n == len(passes) - 1),
                 )
-            y_sb = ring.tile([P, W], F32, name="y_sb", bufs=4)
+            y_sb = ring.tile([P, width], F32, name="y_sb", bufs=4)
             nc.scalar.copy(out=y_sb[:], in_=y[:])
             return y_sb
 
@@ -262,7 +268,7 @@ def tile_list_block_bid_features_kernel(
             if step + 1 < 8:
                 cosines[step + 1] = cosine_of(step + 1, "vector" if step + 1 < 4 else "scalar")
             if step in (5, 6):
-                z_first.append(z1_of(0, len(z_first), "vector", "vector"))
+                z_first.append(z1_of(0, len(z_first), *(("vector","vector"),("scalar","vector"))[len(z_first)]))
             h1_of(step, cosines[step])
 
         v2_w = []
@@ -283,7 +289,31 @@ def tile_list_block_bid_features_kernel(
         for i in range(4):
             place_y1(y1_of(z_first, i), 0, i)
 
-        for b in range(2):
+        half = PB
+
+        def z2_of(part, b):
+            return quantised_z(peaks[b][:, :, half * part : half * (part + 1)], b, "scalar", "scalar")
+
+        def place_y2(z, part, i):
+            cols = slice(P * i, P * (i + 1))
+            bids = slice(half * part, half * (part + 1))
+            y_sb = product(
+                [
+                    (w6_w[a][:, cols].bitcast(E4M3), w6_s[4 * a : P, cols],
+                     v2_w[a][:, bids].bitcast(E4M3), v2_s[4 * a : P, bids])
+                    for a in range(2)
+                ]
+                + [
+                    (w5_q[a][0][:, cols].bitcast(E4M3), w5_q[a][1][:, cols],
+                     z[a][0][:].bitcast(E4M3), z[a][1][:])
+                    for a in range(2)
+                ]
+            )
+            nc.vector.tensor_tensor(
+                pages[i][:].indirect(idx4[:]), y_sb[:], wg2_sb[:, bids], ALU.mult
+            )
+
+        def meet_peaks(b):
             w3_q = [
                 quantised_weight(
                     "w3_%d_%d" % (a, b),
@@ -305,11 +335,13 @@ def tile_list_block_bid_features_kernel(
                     )
                 nc.vector.tensor_tensor(peaks[b][:, t, :], acc[:], peaks[b][:, t, :], ALU.max)
 
+        meet_peaks(0)
+        meet_peaks(1)
         z_second = [z1_of(1, b, "scalar", "scalar") for b in range(2)]
         w5_q = [
             quantised_weight(
                 "w5_%d" % a,
-                interleave(load_raw(w5, a, slice(0, N), "slab%d" % (4 + a)), "scalar", "w_grouped"),
+                interleave(load_raw(w5, a, slice(0, N), "slab%d" % (4 + a))[:], "scalar", "w_grouped", 3),
             )
             for a in range(2)
         ]
@@ -317,22 +349,8 @@ def tile_list_block_bid_features_kernel(
         z_third = []
         for i in range(4):
             place_y1(y1_of(z_second, i), 1, i)
-            if i in (0, 1):
-                b = len(z_third)
-                z_third.append(quantised_z(peaks[b], b, "scalar", "scalar"))
+            if i < 2:
+                z_third.append(z2_of(0, i))
         for i in range(4):
-            cols = slice(P * i, P * (i + 1))
-            y_sb = product(
-                [
-                    (w6_w[a][:, cols].bitcast(E4M3), w6_s[4 * a : P, cols],
-                     v2_w[a][:].bitcast(E4M3), v2_s[4 * a : P, :])
-                    for a in range(2)
-                ]
-                + [
-                    (w5_q[a][0][:, cols].bitcast(E4M3), w5_q[a][1][:, cols],
-                     z_third[a][0][:].bitcast(E4M3), z_third[a][1][:])
-                    for a in range(2)
-                ]
-            )
-            nc.vector.tensor_tensor(pages[i][:].indirect(idx4[:]), y_sb[:], wg2_sb[:], ALU.mult)
+            place_y2(z_third, 0, i)
             nc.sync.dma_start(out=out[P * i : P * (i + 1), :], in_=pages[i][:])

@@ -120,17 +120,17 @@ def tile_list_block_bid_features_kernel(
         w1_raw = [load_raw(w1, 0, slice(W * b, W * (b + 1)), "slab%d" % (1 + b)) for b in range(2)]
         gain_sb = load("gain_sb", [P, 2, 4], F32, gain.rearrange("(b p t) -> p b t", b=2, t=4))
         idx2 = load_list("idx2", offs2)
-        tab2_w = [load_words("tab2_w%d" % a, tab2_words[a], "slab%d" % a) for a in range(2)]
-        tab2_s = load_stacked_scales("tab2_s", tab2_scales, nc.gpsimd, nc.gpsimd)
+        tab2_w = [load_words("tab2_w%d" % a, tab2_words[a], "slab%d" % (1 + a)) for a in range(2)]
+        tab2_s = load_stacked_scales("tab2_s", tab2_scales, nc.sync, nc.gpsimd)
         w4_w = [load("w4_w%d" % a, [P, N // 2], I32, w4_words[a].bitcast(I32)) for a in range(2)]
         w4_s = keep("w4_s", [P, 2, N], U8)
         nc.gpsimd.memset(w4_s[:].bitcast(I32), 0)
         for q in range(4):
-            nc.gpsimd.dma_start(
+            nc.sync.dma_start(
                 out=w4_s[32 * q : 32 * q + 4, :, :].bitcast(I32),
                 in_=w4_scales[:, 4 * q : 4 * q + 4, :].rearrange("a r n -> r a n").bitcast(I32),
             )
-        w6_s = load_stacked_scales("w6_s", w6_scales, nc.gpsimd, nc.gpsimd)
+        w6_s = load_stacked_scales("w6_s", w6_scales, nc.sync, nc.gpsimd)
         idx3 = load_list("idx3", offs3)
         wg1_sb = load("wg1_sb", [P, S], F32, wg1)
         pages = [load("page%d" % i, [P, TO], F32, page1[P * i : P * (i + 1), :], "slab%d" % i) for i in range(4)]
@@ -172,9 +172,10 @@ def tile_list_block_bid_features_kernel(
         def cosine_of(step, whole_on):
             c, b, pair = step // 4, step // 2 % 2, step % 2
             turns = ring.tile([P, 2, W], F32, name="turns", bufs=4)
+            angles = []
             for e in range(2):
                 col0 = W * b + P * (2 * pair + e)
-                x = psum.tile([P, W], F32, name="x", bufs=2)
+                x = psum.tile([P, W], F32, name="x", tag="xy", bufs=5)
                 nc.tensor.matmul_mx(
                     out=x[:],
                     lhsT=w2d_w[:, 2 * col0 : 2 * (col0 + P)].bitcast(E2M1),
@@ -184,16 +185,14 @@ def tile_list_block_bid_features_kernel(
                     start=True,
                     stop=True,
                 )
-                nc.scalar.activation(turns[:, e, :], x[:], ACT.Abs, scale=1.0 / (2.0 * math.pi))
-            if whole_on == "scalar":
-                whole = ring.tile([P, 2, W], U32, name="whole", bufs=2)
-                nc.scalar.activation(whole[:], turns[:], ACT.Identity, bias=0.25)
-                whole_int = whole[:].bitcast(I32)
-            else:
-                whole = ring.tile([P, 2, W], I32, name="whole", bufs=2)
-                nc.vector.tensor_scalar(whole[:], turns[:], 0.25, None, ALU.add)
-                whole_int = whole[:]
-            nc.vector.tensor_tensor(turns[:], turns[:], whole_int, ALU.subtract)
+                nc.scalar.activation(turns[:, e, :], x[:], ACT.Copy, scale=1.0 / (2.0 * math.pi))
+                angles.append(x)
+            whole = ring.tile([P, 2, W], I32, name="whole", bufs=2)
+            nc.gpsimd.tensor_scalar(whole[:], turns[:], 1.0, 0.25, ALU.mult, ALU.add)
+            for e in range(2):
+                nc.vector.scalar_tensor_tensor(
+                    turns[:, e, :], angles[e][:], 1.0 / (2.0 * math.pi), whole[:, e, :], ALU.mult, ALU.subtract
+                )
             nc.scalar.activation(turns[:], turns[:], ACT.Sin, scale=2.0 * math.pi, bias=0.5 * math.pi)
             return turns
 
@@ -213,20 +212,33 @@ def tile_list_block_bid_features_kernel(
                 )
                 nc.vector.tensor_tensor(h1[b][:, t, W * c : W * (c + 1)], acc[:], cosine[:, e, :], ALU.add)
 
-        def quantised_z(pre, b, gain_on, weave_on):
+        def with_gain(pre, b, gain_on):
             width = pre.shape[2]
             rounded = ring.tile([P, 4, width], BF16, name="rounded", bufs=2)
             for t in range(4):
                 factor = gain_sb[:, b, t : t + 1]
                 if gain_on == "scalar":
                     nc.scalar.activation(rounded[:, t, :], pre[:, t, :], ACT.Copy, scale=factor)
+                elif gain_on == "gpsimd":
+                    nc.gpsimd.tensor_scalar(rounded[:, t, :], pre[:, t, :], factor, 0.0, ALU.mult, ALU.add)
                 else:
                     nc.vector.tensor_scalar(rounded[:, t, :], pre[:, t, :], factor, None, ALU.mult)
+            return rounded
+
+        def quantised_rows(rounded, weave_on):
+            width = rounded.shape[2]
             grouped = interleave(rounded[:], weave_on, "z_grouped")
             codes = ring.tile([P, width], U32, name="z_codes", bufs=4, align_bytes=64)
             scales = ring.tile([P, width], U8, name="z_scales", bufs=4, align_bytes=64)
             quantise(grouped, codes, scales)
             return codes, scales
+
+        def quantised_z(pre, b, gain_on, weave_on):
+            return quantised_rows(with_gain(pre, b, gain_on), weave_on)
+
+        def w5_of(a):
+            raw = load_raw(w5, a, slice(0, N), "slab%d" % (4 + a))
+            return quantised_weight("w5_%d" % a, interleave(raw[:], "scalar", "w_grouped", 3))
 
         def z1_of(c, b, gain_on, weave_on):
             pre = ring.tile([P, 4, W], F32, name="pre", bufs=2)
@@ -235,7 +247,7 @@ def tile_list_block_bid_features_kernel(
 
         def product(passes):
             width = passes[0][2].shape[1]
-            y = psum.tile([P, width], F32, name="y", bufs=3)
+            y = psum.tile([P, width], F32, name="y", tag="xy", bufs=5)
             for n, (lw, ls, rw, rs) in enumerate(passes):
                 nc.tensor.matmul_mx(
                     out=y[:], lhsT=lw, lhsT_scale=ls, rhs=rw, rhs_scale=rs,
@@ -267,8 +279,8 @@ def tile_list_block_bid_features_kernel(
         for step in range(8):
             if step + 1 < 8:
                 cosines[step + 1] = cosine_of(step + 1, "vector" if step + 1 < 4 else "scalar")
-            if step in (5, 6):
-                z_first.append(z1_of(0, len(z_first), *(("vector","vector"),("scalar","vector"))[len(z_first)]))
+            if step in (3, 5):
+                z_first.append(z1_of(0, len(z_first), *(("gpsimd","scalar"),("gpsimd","scalar"))[len(z_first)]))
             h1_of(step, cosines[step])
 
         v2_w = []
@@ -279,13 +291,23 @@ def tile_list_block_bid_features_kernel(
         v2_s = keep("v2_s", [P, PB], U8)
         nc.vector.tensor_copy(v2_s[:], tab2_s[:].indirect(idx2[:]))
 
-        peaks = []
-        for b in range(2):
-            pre = ring.tile([P, 4, W], F32, name="peaks", bufs=2)
+        def w3_of(b):
+            return [
+                quantised_weight(
+                    "w3_%d_%d" % (a, b),
+                    round_dealt(load_raw(w3, a, slice(W * b, W * (b + 1)), "slab%d" % (6 - 2 * b + a)), "scalar"),
+                )
+                for a in range(2)
+            ]
+
+        def peaks_of(b):
+            pre = held.tile([P, 4, W], F32, name="peaks", tag="slab%d" % (6 + b), align_bytes=64)
             for t in range(4):
                 nc.vector.tensor_copy(pre[:, t, :], h1[b][:, t, :].indirect(peak[:]))
-            peaks.append(pre)
+            return pre
 
+        w3_first = w3_of(0)
+        peaks = [peaks_of(b) for b in range(2)]
         for i in range(4):
             place_y1(y1_of(z_first, i), 0, i)
 
@@ -314,13 +336,7 @@ def tile_list_block_bid_features_kernel(
             )
 
         def meet_peaks(b):
-            w3_q = [
-                quantised_weight(
-                    "w3_%d_%d" % (a, b),
-                    round_dealt(load_raw(w3, a, slice(W * b, W * (b + 1)), "slab%d" % (4 + a)), "scalar"),
-                )
-                for a in range(2)
-            ]
+            w3_q = w3_first if b == 0 else w3_of(1)
             for t in range(4):
                 acc = psum.tile([P, W], F32, name="acc", bufs=3)
                 for a in range(2):
@@ -336,21 +352,17 @@ def tile_list_block_bid_features_kernel(
                 nc.vector.tensor_tensor(peaks[b][:, t, :], acc[:], peaks[b][:, t, :], ALU.max)
 
         meet_peaks(0)
-        meet_peaks(1)
         z_second = [z1_of(1, b, "scalar", "scalar") for b in range(2)]
-        w5_q = [
-            quantised_weight(
-                "w5_%d" % a,
-                interleave(load_raw(w5, a, slice(0, N), "slab%d" % (4 + a))[:], "scalar", "w_grouped", 3),
-            )
-            for a in range(2)
-        ]
-
+        place_y1(y1_of(z_second, 0), 1, 0)
+        meet_peaks(1)
         z_third = []
-        for i in range(4):
-            place_y1(y1_of(z_second, i), 1, i)
-            if i < 2:
-                z_third.append(z2_of(0, i))
+        w5_q = []
+        for b in range(2):
+            place_y1(y1_of(z_second, 1 + b), 1, 1 + b)
+            rounded = with_gain(peaks[b][:], b, "scalar")
+            w5_q.append(w5_of(b))
+            z_third.append(quantised_rows(rounded, "scalar"))
+        place_y1(y1_of(z_second, 3), 1, 3)
         for i in range(4):
             place_y2(z_third, 0, i)
             nc.sync.dma_start(out=out[P * i : P * (i + 1), :], in_=pages[i][:])

@@ -3,8 +3,8 @@ from contextlib import ExitStack
 
 import concourse.mybir as mybir
 
-K, K2, H, N, T, S, PB, TO = 512, 1024, 1024, 512, 2048, 1024, 512, 2048
-FLOPS = 2 * (2 * K * H * S + K2 * H * PB + H * N * S + H * N * PB + K2 * N * PB)
+K, K2, H, N, S, BIDS, SLOTS = 512, 1024, 1024, 512, 1024, 512, 2048
+FLOPS = 2 * (2 * K * H * S + K2 * H * BIDS + H * N * S + H * N * BIDS + K2 * N * BIDS)
 
 F32 = mybir.dt.float32
 BF16 = mybir.dt.bfloat16
@@ -19,7 +19,10 @@ ACT = mybir.ActivationFunctionType
 
 P = 128
 W = 512
-LCOLS = W // 16
+LIST_COLS = W // 16
+PER_TURN = 1.0 / (2.0 * math.pi)
+Z1_STEPS = (3, 5)
+STEPS = 8
 
 
 def tile_list_block_bid_features_kernel(
@@ -31,39 +34,34 @@ def tile_list_block_bid_features_kernel(
     with ExitStack() as ctx:
         held = ctx.enter_context(tc.tile_pool(name="held", bufs=1))
         ring = ctx.enter_context(tc.tile_pool(name="ring", bufs=2))
-        psum = ctx.enter_context(tc.psum_pool(name="psum", bufs=2))
+        psum = ctx.enter_context(tc.psum_pool(name="psum", bufs=1))
 
-        def keep(name, shape, dtype):
-            return held.tile(shape, dtype, name=name, align_bytes=64)
+        def keep(name, shape, dtype, buffer=None):
+            return held.tile(shape, dtype, name=name, tag=buffer or name, align_bytes=64)
+
+        def slab(n):
+            return "slab%d" % n
+
+        def load(name, shape, dtype, src, buffer=None):
+            dst = keep(name, shape, dtype, buffer)
+            nc.sync.dma_start(out=dst[:], in_=src)
+            return dst
 
         def load_list(name, src):
             lst = held.tile(list(src.shape), U16, name=name)
             nc.sync.dma_start(lst[:], src)
             return lst
 
-        def load(name, shape, dtype, src, tag=None):
-            dst = held.tile(shape, dtype, name=name, tag=tag or name, align_bytes=64)
-            nc.sync.dma_start(out=dst[:], in_=src)
-            return dst
-
-        def load_words(name, words, tag=None):
+        def load_words(name, words, buffer=None):
             flat = words.rearrange("p c i -> p (c i)").bitcast(I32)
-            return load(name, list(flat.shape), I32, flat, tag)
+            return load(name, list(flat.shape), I32, flat, buffer)
 
-        def load_stacked_scales(name, scales, queue, zero):
-            passes, rows, width = scales.shape
-            plane = keep(name, [P, width], U8)
-            zero.memset(plane[:].bitcast(I32), 0)
-            for q in range(4):
-                queue.dma_start(
-                    out=plane[32 * q : 32 * q + 4 * passes, :].bitcast(I32),
-                    in_=scales[:, 4 * q : 4 * q + 4, :].bitcast(I32),
-                )
-            return plane
+        def load_rows(w, a, cols, buffer):
+            rows = w[W * a : W * (a + 1), cols].rearrange("(p j) c -> p j c", j=4)
+            return load("rows", [P, 4, W], F32, rows, buffer)
 
         def load_repeated_scales(name, scales):
-            rows, width = scales.shape
-            plane = keep(name, [P, width], U8)
+            plane = keep(name, [P, scales.shape[1]], U8)
             for q in range(4):
                 nc.sync.dma_start(
                     out=plane[32 * q : 32 * (q + 1), :].bitcast(I32),
@@ -71,42 +69,68 @@ def tile_list_block_bid_features_kernel(
                 )
             return plane
 
-        def load_raw(w, a, cols, tag):
-            rows = w[W * a : W * (a + 1), cols].rearrange("(p j) c -> p j c", j=4)
-            return load("raw", [P, 4, W], F32, rows, tag)
+        def load_stacked_scales(name, scales):
+            plane = keep(name, [P, scales.shape[2]], U8)
+            nc.gpsimd.memset(plane[:].bitcast(I32), 0)
+            for q in range(4):
+                nc.sync.dma_start(
+                    out=plane[32 * q : 32 * q + 8, :].bitcast(I32),
+                    in_=scales[:, 4 * q : 4 * q + 4, :].bitcast(I32),
+                )
+            return plane
 
-        def copy_on(engine, dst, src):
-            if engine == "scalar":
-                nc.scalar.copy(out=dst, in_=src)
-            else:
-                nc.vector.tensor_copy(out=dst, in_=src)
+        def load_adjacent_scales(name, scales):
+            plane = keep(name, [P, 2, scales.shape[2]], U8)
+            nc.gpsimd.memset(plane[:].bitcast(I32), 0)
+            for q in range(4):
+                nc.sync.dma_start(
+                    out=plane[32 * q : 32 * q + 4, :, :].bitcast(I32),
+                    in_=scales[:, 4 * q : 4 * q + 4, :].rearrange("a r n -> r a n").bitcast(I32),
+                )
+            return plane
+
+        def weight_staging():
+            return ring.tile([P, 4 * W], BF16, name="w_grouped", bufs=3, align_bytes=64)
+
+        def round_dealt(rows, copy):
+            grouped = weight_staging()
+            copy(
+                out=grouped[:].rearrange("p (t m j) -> p m j t", t=4, j=4),
+                in_=rows[:].rearrange("p j (m t) -> p m j t", t=4),
+            )
+            return grouped
+
+        def interleave(grouped, rows, copy):
+            copy(
+                out=grouped[:].rearrange("p (c i j) -> p c j i", i=4, j=4),
+                in_=rows[:].rearrange("p j (c i) -> p c j i", i=4),
+            )
+            return grouped
 
         def quantise(grouped, codes, scales):
             nc.vector.quantize_mx(out=codes[:].bitcast(E4M3), scales=scales[:], in_=grouped[:])
-
-        def round_dealt(raw, engine):
-            grouped = ring.tile([P, 4 * W], BF16, name="w_grouped", bufs=3, align_bytes=64)
-            copy_on(
-                engine,
-                grouped[:].rearrange("p (t m j) -> p m j t", t=4, j=4),
-                raw[:].rearrange("p j (m t) -> p m j t", t=4),
-            )
-            return grouped
-
-        def interleave(rows, engine, name, bufs=2):
-            grouped = ring.tile([P, 4 * rows.shape[2]], BF16, name=name, bufs=bufs, align_bytes=64)
-            copy_on(
-                engine,
-                grouped[:].rearrange("p (c i j) -> p c j i", i=4, j=4),
-                rows.rearrange("p j (c i) -> p c j i", i=4),
-            )
-            return grouped
-
-        def quantised_weight(name, grouped):
-            codes = keep(name + "_codes", [P, W], U32)
-            scales = keep(name + "_scales", [P, W], U8)
-            quantise(grouped, codes, scales)
             return codes, scales
+
+        def quantise_weight(name, grouped):
+            return quantise(grouped, keep(name + "_codes", [P, W], U32), keep(name + "_scales", [P, W], U8))
+
+        def multiply(acc, passes):
+            for n, (lhs_words, lhs_scales, rhs_words, rhs_scales) in enumerate(passes):
+                nc.tensor.matmul_mx(
+                    out=acc[:], lhsT=lhs_words, lhsT_scale=lhs_scales, rhs=rhs_words, rhs_scale=rhs_scales,
+                    start=(n == 0), stop=(n == len(passes) - 1),
+                )
+            return acc
+
+        def scalar_bank():
+            return psum.tile([P, W], F32, name="scalar_bank", bufs=5)
+
+        def vector_bank():
+            return psum.tile([P, W], F32, name="vector_bank", bufs=3)
+
+        def stationary(quantised, n):
+            cols = slice(P * n, P * (n + 1))
+            return quantised[0][:, cols].bitcast(E4M3), quantised[1][:, cols]
 
         warm = keep("warm", [P, 1], F32)
         nc.vector.memset(warm[:], 0.0)
@@ -115,40 +139,29 @@ def tile_list_block_bid_features_kernel(
         idx = load_list("idx", offs)
         tab_s = load_repeated_scales("tab_s", tab_scales[0])
         w2_w = load("w2_w", [P, H // 2], I32, w2_words[0].bitcast(I32))
-        tab_w = load_words("tab_w", tab_words[0], "slab0")
+        tab_w = load_words("tab_w", tab_words[0], slab(0))
         w2_s = load_repeated_scales("w2_s", w2_scales[0])
-        w1_raw = [load_raw(w1, 0, slice(W * b, W * (b + 1)), "slab%d" % (1 + b)) for b in range(2)]
+        w1_rows = [load_rows(w1, 0, slice(W * b, W * (b + 1)), slab(1 + b)) for b in range(2)]
         gain_sb = load("gain_sb", [P, 2, 4], F32, gain.rearrange("(b p t) -> p b t", b=2, t=4))
         idx2 = load_list("idx2", offs2)
-        tab2_w = [load_words("tab2_w%d" % a, tab2_words[a], "slab%d" % (1 + a)) for a in range(2)]
-        tab2_s = load_stacked_scales("tab2_s", tab2_scales, nc.sync, nc.gpsimd)
-        w4_w = [load("w4_w%d" % a, [P, N // 2], I32, w4_words[a].bitcast(I32)) for a in range(2)]
-        w4_s = keep("w4_s", [P, 2, N], U8)
-        nc.gpsimd.memset(w4_s[:].bitcast(I32), 0)
-        for q in range(4):
-            nc.sync.dma_start(
-                out=w4_s[32 * q : 32 * q + 4, :, :].bitcast(I32),
-                in_=w4_scales[:, 4 * q : 4 * q + 4, :].rearrange("a r n -> r a n").bitcast(I32),
-            )
-        w6_s = load_stacked_scales("w6_s", w6_scales, nc.sync, nc.gpsimd)
+        peak_idx = load_list("peak_idx", pos1)
         idx3 = load_list("idx3", offs3)
-        wg1_sb = load("wg1_sb", [P, S], F32, wg1)
-        pages = [load("page%d" % i, [P, TO], F32, page1[P * i : P * (i + 1), :], "slab%d" % i) for i in range(4)]
-        peak = load_list("peak", pos1)
         idx4 = load_list("idx4", offs4)
-        wg2_sb = load("wg2_sb", [P, PB], F32, wg2)
+        tab2_s = load_stacked_scales("tab2_s", tab2_scales)
+        tab2_w = [load_words("tab2_w%d" % a, tab2_words[a], slab(6 + a)) for a in range(2)]
+        w4_w = [load("w4_w%d" % a, [P, N // 2], I32, w4_words[a].bitcast(I32)) for a in range(2)]
+        w4_s = load_adjacent_scales("w4_s", w4_scales)
+        wg1_sb = load("wg1_sb", [P, S], F32, wg1)
+
+        def load_page(i):
+            return load("page%d" % i, [P, SLOTS], F32, page1[P * i : P * (i + 1), :], slab(i))
+
+        pages = [load_page(i) for i in range(2)]
+        w3_rows = [load_rows(w3, a, slice(0, W), slab(4 + a)) for a in range(2)]
+        pages.extend([load_page(i) for i in range(2, 4)])
+        w6_s = load_stacked_scales("w6_s", w6_scales)
         w6_w = [load_words("w6_w%d" % a, w6_words[a]) for a in range(2)]
-
-        v_w, v_s = [], []
-
-        def gather_v(c):
-            part = idx[:, LCOLS * c : LCOLS * (c + 1)]
-            words = held.tile([P, W], U32, name="v_w%d" % c, tag="v_w0" if c == 0 else "w2_s", align_bytes=64)
-            scales = keep("v_s%d" % c, [P, W], U8)
-            nc.vector.tensor_copy(words[:], tab_w[:].bitcast(U32).indirect(part))
-            nc.vector.tensor_copy(scales[:], tab_s[:].indirect(part))
-            v_w.append(words)
-            v_s.append(scales)
+        wg2_sb = load("wg2_sb", [P, BIDS], F32, wg2)
 
         w2d_w = keep("w2d_w", [P, 2 * H], U8)
         w2d_s = keep("w2d_s", [P, H], U8)
@@ -160,209 +173,167 @@ def tile_list_block_bid_features_kernel(
             out=w2d_s[:].rearrange("p (b t m) -> p b m t", b=2, t=4),
             in_=w2_s[:].rearrange("p (b m t) -> p b m t", b=2, t=4),
         )
-        gather_v(0)
+
+        def hours_of(c, buffer):
+            entries = idx[:, LIST_COLS * c : LIST_COLS * (c + 1)]
+            words = keep("v_w%d" % c, [P, W], U32, buffer)
+            scales = keep("v_s%d" % c, [P, W], U8)
+            nc.vector.tensor_copy(words[:], tab_w[:].bitcast(U32).indirect(entries))
+            nc.vector.tensor_copy(scales[:], tab_s[:].indirect(entries))
+            return words[:].bitcast(E4M3), scales[:]
+
+        hours = [hours_of(0, None)]
         w1_q = [
-            quantised_weight("w1_%d" % b, round_dealt(w1_raw[b], "vector" if b == 0 else "scalar"))
-            for b in range(2)
+            quantise_weight("w1_%d" % b, round_dealt(w1_rows[b], copy))
+            for b, copy in enumerate((nc.vector.tensor_copy, nc.scalar.copy))
         ]
-        gather_v(1)
+        hours.append(hours_of(1, "w2_s"))
 
         h1 = [keep("h1_%d" % b, [P, 4, S], F32) for b in range(2)]
 
-        def cosine_of(step, whole_on):
-            c, b, pair = step // 4, step // 2 % 2, step % 2
-            turns = ring.tile([P, 2, W], F32, name="turns", bufs=4)
+        def cosine_of(step):
+            c, first = step // 4, 2 * (step % 4)
+            turns = keep("turns", [P, 2, W], F32, "turns%d" % (step % 4))
             angles = []
             for e in range(2):
-                col0 = W * b + P * (2 * pair + e)
-                x = psum.tile([P, W], F32, name="x", tag="xy", bufs=5)
-                nc.tensor.matmul_mx(
-                    out=x[:],
-                    lhsT=w2d_w[:, 2 * col0 : 2 * (col0 + P)].bitcast(E2M1),
-                    lhsT_scale=w2d_s[:, col0 : col0 + P],
-                    rhs=v_w[c][:].bitcast(E4M3),
-                    rhs_scale=v_s[c][:],
-                    start=True,
-                    stop=True,
-                )
-                nc.scalar.activation(turns[:, e, :], x[:], ACT.Copy, scale=1.0 / (2.0 * math.pi))
-                angles.append(x)
+                col = P * (first + e)
+                w2_pass = (w2d_w[:, 2 * col : 2 * (col + P)].bitcast(E2M1), w2d_s[:, col : col + P])
+                angles.append(multiply(scalar_bank(), [w2_pass + hours[c]]))
+                nc.scalar.activation(turns[:, e, :], angles[e][:], ACT.Copy, scale=PER_TURN)
             whole = ring.tile([P, 2, W], I32, name="whole", bufs=2)
             nc.gpsimd.tensor_scalar(whole[:], turns[:], 1.0, 0.25, ALU.mult, ALU.add)
             for e in range(2):
                 nc.vector.scalar_tensor_tensor(
-                    turns[:, e, :], angles[e][:], 1.0 / (2.0 * math.pi), whole[:, e, :], ALU.mult, ALU.subtract
+                    turns[:, e, :], angles[e][:], PER_TURN, whole[:, e, :], ALU.mult, ALU.subtract
                 )
             nc.scalar.activation(turns[:], turns[:], ACT.Sin, scale=2.0 * math.pi, bias=0.5 * math.pi)
             return turns
 
         def h1_of(step, cosine):
-            c, b, pair = step // 4, step // 2 % 2, step % 2
+            c, b, first = step // 4, step // 2 % 2, 2 * (step % 2)
             for e in range(2):
-                t = 2 * pair + e
-                acc = psum.tile([P, W], F32, name="acc", bufs=3)
-                nc.tensor.matmul_mx(
-                    out=acc[:],
-                    lhsT=w1_q[b][0][:, P * t : P * (t + 1)].bitcast(E4M3),
-                    lhsT_scale=w1_q[b][1][:, P * t : P * (t + 1)],
-                    rhs=v_w[c][:].bitcast(E4M3),
-                    rhs_scale=v_s[c][:],
-                    start=True,
-                    stop=True,
+                acc = multiply(vector_bank(), [stationary(w1_q[b], first + e) + hours[c]])
+                nc.vector.tensor_tensor(
+                    h1[b][:, first + e, W * c : W * (c + 1)], acc[:], cosine[:, e, :], ALU.add
                 )
-                nc.vector.tensor_tensor(h1[b][:, t, W * c : W * (c + 1)], acc[:], cosine[:, e, :], ALU.add)
 
-        def with_gain(pre, b, gain_on):
-            width = pre.shape[2]
-            rounded = ring.tile([P, 4, width], BF16, name="rounded", bufs=2)
+        def tanh_of(c, b):
+            tanh = ring.tile([P, 4, W], F32, name="tanh", bufs=2)
+            nc.scalar.activation(tanh[:], h1[b][:, :, W * c : W * (c + 1)], ACT.Tanh)
+            return tanh
+
+        def gain_on_gpsimd(dst, src, factor):
+            nc.gpsimd.tensor_scalar(dst, src, factor, 0.0, ALU.mult, ALU.add)
+
+        def copy_on_gpsimd(out, in_):
+            nc.gpsimd.tensor_scalar(out, in_, 1.0, 0.0, ALU.mult, ALU.add)
+
+        def gain_on_scalar(dst, src, factor):
+            nc.scalar.activation(dst, src, ACT.Copy, scale=factor)
+
+        def with_gain(values, b, apply_gain):
+            rounded = ring.tile([P, 4, W], BF16, name="rounded", bufs=2)
             for t in range(4):
-                factor = gain_sb[:, b, t : t + 1]
-                if gain_on == "scalar":
-                    nc.scalar.activation(rounded[:, t, :], pre[:, t, :], ACT.Copy, scale=factor)
-                elif gain_on == "gpsimd":
-                    nc.gpsimd.tensor_scalar(rounded[:, t, :], pre[:, t, :], factor, 0.0, ALU.mult, ALU.add)
-                else:
-                    nc.vector.tensor_scalar(rounded[:, t, :], pre[:, t, :], factor, None, ALU.mult)
+                apply_gain(rounded[:, t, :], values[:, t, :], gain_sb[:, b, t : t + 1])
             return rounded
 
-        def quantised_rows(rounded, weave_on):
-            width = rounded.shape[2]
-            grouped = interleave(rounded[:], weave_on, "z_grouped")
-            codes = ring.tile([P, width], U32, name="z_codes", bufs=4, align_bytes=64)
-            scales = ring.tile([P, width], U8, name="z_scales", bufs=4, align_bytes=64)
+        def group_z(rounded, copy):
+            grouped = ring.tile([P, 4 * W], BF16, name="z_grouped", bufs=2, align_bytes=64)
+            return interleave(grouped, rounded, copy)
+
+        def z_codes():
+            return ring.tile([P, W], U32, name="z_codes", bufs=4, align_bytes=64)
+
+        def quantise_z(grouped, codes):
+            scales = ring.tile([P, W], U8, name="z_scales", bufs=4, align_bytes=64)
             quantise(grouped, codes, scales)
-            return codes, scales
+            return codes[:].bitcast(E4M3), scales[:]
 
-        def quantised_z(pre, b, gain_on, weave_on):
-            return quantised_rows(with_gain(pre, b, gain_on), weave_on)
+        def place(passes, i, entries, factors):
+            y = ring.tile([P, W], F32, name="y", bufs=4)
+            nc.scalar.copy(out=y[:], in_=multiply(scalar_bank(), passes)[:])
+            nc.vector.tensor_tensor(pages[i][:].indirect(entries), y[:], factors, ALU.mult)
 
-        def w5_of(a):
-            raw = load_raw(w5, a, slice(0, N), "slab%d" % (4 + a))
-            return quantised_weight("w5_%d" % a, interleave(raw[:], "scalar", "w_grouped", 3))
-
-        def z1_of(c, b, gain_on, weave_on):
-            pre = ring.tile([P, 4, W], F32, name="pre", bufs=2)
-            nc.scalar.activation(pre[:], h1[b][:, :, W * c : W * (c + 1)], ACT.Tanh)
-            return quantised_z(pre[:], b, gain_on, weave_on)
-
-        def product(passes):
-            width = passes[0][2].shape[1]
-            y = psum.tile([P, width], F32, name="y", tag="xy", bufs=5)
-            for n, (lw, ls, rw, rs) in enumerate(passes):
-                nc.tensor.matmul_mx(
-                    out=y[:], lhsT=lw, lhsT_scale=ls, rhs=rw, rhs_scale=rs,
-                    start=(n == 0), stop=(n == len(passes) - 1),
-                )
-            y_sb = ring.tile([P, width], F32, name="y_sb", bufs=4)
-            nc.scalar.copy(out=y_sb[:], in_=y[:])
-            return y_sb
-
-        def y1_of(z, i):
-            return product([
-                (
-                    w4_w[a][:].bitcast(U8)[:, 2 * P * i : 2 * P * (i + 1)].bitcast(E2M1),
-                    w4_s[:, a, P * i : P * (i + 1)],
-                    z[a][0][:].bitcast(E4M3),
-                    z[a][1][:],
-                )
+        def place_y1(z1, c, i):
+            passes = [
+                (w4_w[a][:].bitcast(U8)[:, 2 * P * i : 2 * P * (i + 1)].bitcast(E2M1), w4_s[:, a, P * i : P * (i + 1)])
+                + z1[a]
                 for a in range(2)
-            ])
+            ]
+            place(passes, i, idx3[:, LIST_COLS * c : LIST_COLS * (c + 1)], wg1_sb[:, W * c : W * (c + 1)])
 
-        def place_y1(y_sb, c, i):
-            nc.vector.tensor_tensor(
-                pages[i][:].indirect(idx3[:, LCOLS * c : LCOLS * (c + 1)]),
-                y_sb[:], wg1_sb[:, W * c : W * (c + 1)], ALU.mult,
-            )
+        grouped_first = []
+        cosine = cosine_of(0)
+        for step in range(STEPS):
+            next_cosine = cosine_of(step + 1) if step + 1 < STEPS else None
+            if step in Z1_STEPS:
+                b = len(grouped_first)
+                grouped_first.append(group_z(with_gain(tanh_of(0, b), b, gain_on_gpsimd), nc.scalar.copy))
+            h1_of(step, cosine)
+            cosine = next_cosine
 
-        z_first = []
-        cosines = {0: cosine_of(0, "vector")}
-        for step in range(8):
-            if step + 1 < 8:
-                cosines[step + 1] = cosine_of(step + 1, "vector" if step + 1 < 4 else "scalar")
-            if step in (3, 5):
-                z_first.append(z1_of(0, len(z_first), *(("gpsimd","scalar"),("gpsimd","scalar"))[len(z_first)]))
-            h1_of(step, cosines[step])
+        last_buffer = "turns%d" % ((STEPS - 1) % 4)
+        z1_first = [
+            quantise_z(grouped_first[0], z_codes()),
+            quantise_z(grouped_first[1], keep("held_codes", [P, W], U32, last_buffer)),
+        ]
 
-        v2_w = []
+        v2_s = keep("v2_s", [P, BIDS], U8)
+        bids = []
         for a in range(2):
-            words = keep("v2_w%d" % a, [P, PB], U32)
+            words = keep("v2_w%d" % a, [P, BIDS], U32)
             nc.vector.tensor_copy(words[:], tab2_w[a][:].bitcast(U32).indirect(idx2[:]))
-            v2_w.append(words)
-        v2_s = keep("v2_s", [P, PB], U8)
+            bids.append((words[:].bitcast(E4M3), v2_s[4 * a : P, :]))
         nc.vector.tensor_copy(v2_s[:], tab2_s[:].indirect(idx2[:]))
 
         def w3_of(b):
-            return [
-                quantised_weight(
-                    "w3_%d_%d" % (a, b),
-                    round_dealt(load_raw(w3, a, slice(W * b, W * (b + 1)), "slab%d" % (6 - 2 * b + a)), "scalar"),
-                )
-                for a in range(2)
-            ]
+            rows = w3_rows if b == 0 else [load_rows(w3, a, slice(W, 2 * W), "h1_%d" % a) for a in range(2)]
+            return [quantise_weight("w3_%d_%d" % (a, b), round_dealt(rows[a], nc.scalar.copy)) for a in range(2)]
+
+        def w5_of(a):
+            rows = ring.tile([P, 4, W], F32, name="w5_rows", tag="tanh", bufs=2)
+            nc.sync.dma_start(out=rows[:], in_=w5[W * a : W * (a + 1), :].rearrange("(p j) c -> p j c", j=4))
+            return quantise_weight("w5_%d" % a, interleave(weight_staging(), rows, nc.scalar.copy))
 
         def peaks_of(b):
-            pre = held.tile([P, 4, W], F32, name="peaks", tag="slab%d" % (6 + b), align_bytes=64)
+            picked = keep("peaks", [P, 4, W], F32, slab(6 + b))
             for t in range(4):
-                nc.vector.tensor_copy(pre[:, t, :], h1[b][:, t, :].indirect(peak[:]))
-            return pre
+                nc.vector.tensor_copy(picked[:, t, :], h1[b][:, t, :].indirect(peak_idx[:]))
+            return picked
 
-        w3_first = w3_of(0)
-        peaks = [peaks_of(b) for b in range(2)]
-        for i in range(4):
-            place_y1(y1_of(z_first, i), 0, i)
-
-        half = PB
-
-        def z2_of(part, b):
-            return quantised_z(peaks[b][:, :, half * part : half * (part + 1)], b, "scalar", "scalar")
-
-        def place_y2(z, part, i):
-            cols = slice(P * i, P * (i + 1))
-            bids = slice(half * part, half * (part + 1))
-            y_sb = product(
-                [
-                    (w6_w[a][:, cols].bitcast(E4M3), w6_s[4 * a : P, cols],
-                     v2_w[a][:, bids].bitcast(E4M3), v2_s[4 * a : P, bids])
-                    for a in range(2)
-                ]
-                + [
-                    (w5_q[a][0][:, cols].bitcast(E4M3), w5_q[a][1][:, cols],
-                     z[a][0][:].bitcast(E4M3), z[a][1][:])
-                    for a in range(2)
-                ]
-            )
-            nc.vector.tensor_tensor(
-                pages[i][:].indirect(idx4[:]), y_sb[:], wg2_sb[:, bids], ALU.mult
-            )
-
-        def meet_peaks(b):
-            w3_q = w3_first if b == 0 else w3_of(1)
+        def meet_peaks(b, w3_q):
             for t in range(4):
-                acc = psum.tile([P, W], F32, name="acc", bufs=3)
-                for a in range(2):
-                    nc.tensor.matmul_mx(
-                        out=acc[:],
-                        lhsT=w3_q[a][0][:, P * t : P * (t + 1)].bitcast(E4M3),
-                        lhsT_scale=w3_q[a][1][:, P * t : P * (t + 1)],
-                        rhs=v2_w[a][:].bitcast(E4M3),
-                        rhs_scale=v2_s[4 * a : P, :],
-                        start=(a == 0),
-                        stop=(a == 1),
-                    )
+                acc = multiply(vector_bank(), [stationary(w3_q[a], t) + bids[a] for a in range(2)])
                 nc.vector.tensor_tensor(peaks[b][:, t, :], acc[:], peaks[b][:, t, :], ALU.max)
 
-        meet_peaks(0)
-        z_second = [z1_of(1, b, "scalar", "scalar") for b in range(2)]
-        place_y1(y1_of(z_second, 0), 1, 0)
-        meet_peaks(1)
-        z_third = []
-        w5_q = []
+        def place_y2(z2, w5_q, i):
+            cols = slice(P * i, P * (i + 1))
+            passes = [(w6_w[a][:, cols].bitcast(E4M3), w6_s[4 * a : P, cols]) + bids[a] for a in range(2)]
+            passes.extend([stationary(w5_q[a], i) + z2[a] for a in range(2)])
+            place(passes, i, idx4[:], wg2_sb[:])
+
+        peaks = [peaks_of(b) for b in range(2)]
+        for i in range(2):
+            place_y1(z1_first, 0, i)
+        rounded = with_gain(tanh_of(1, 0), 0, gain_on_scalar)
+        tanh = tanh_of(1, 1)
+        z1_second = [quantise_z(group_z(rounded, nc.scalar.copy), z_codes())]
+        place_y1(z1_first, 0, 2)
+        rounded = with_gain(tanh, 1, gain_on_scalar)
+        w3_first = w3_of(0)
+        z1_second.append(quantise_z(group_z(rounded, nc.scalar.copy), z_codes()))
+        place_y1(z1_first, 0, 3)
+        place_y1(z1_second, 1, 0)
+        meet_peaks(0, w3_first)
+        w3_second = w3_of(1)
+        place_y1(z1_second, 1, 1)
+        meet_peaks(1, w3_second)
+        z2, w5_q = [], []
         for b in range(2):
-            place_y1(y1_of(z_second, 1 + b), 1, 1 + b)
-            rounded = with_gain(peaks[b][:], b, "scalar")
+            rounded = with_gain(peaks[b], b, gain_on_scalar)
             w5_q.append(w5_of(b))
-            z_third.append(quantised_rows(rounded, "scalar"))
-        place_y1(y1_of(z_second, 3), 1, 3)
+            z2.append(quantise_z(group_z(rounded, nc.scalar.copy), z_codes()))
+            place_y1(z1_second, 1, 2 + b)
         for i in range(4):
-            place_y2(z_third, 0, i)
+            place_y2(z2, w5_q, i)
             nc.sync.dma_start(out=out[P * i : P * (i + 1), :], in_=pages[i][:])

@@ -21,7 +21,8 @@ P = 128
 W = 512
 LIST_COLS = W // 16
 PER_TURN = 1.0 / (2.0 * math.pi)
-Z1_STEPS = (3, 5)
+Z1_STEPS = (4, 6)
+TURN_BUFFERS = 4
 STEPS = 8
 
 
@@ -100,8 +101,8 @@ def tile_list_block_bid_features_kernel(
             )
             return grouped
 
-        def interleave(grouped, rows, copy):
-            copy(
+        def interleave(grouped, rows):
+            nc.scalar.copy(
                 out=grouped[:].rearrange("p (c i j) -> p c j i", i=4, j=4),
                 in_=rows[:].rearrange("p j (c i) -> p c j i", i=4),
             )
@@ -193,7 +194,7 @@ def tile_list_block_bid_features_kernel(
 
         def cosine_of(step):
             c, first = step // 4, 2 * (step % 4)
-            turns = keep("turns", [P, 2, W], F32, "turns%d" % (step % 4))
+            turns = keep("turns", [P, 2, W], F32, "turns%d" % (step % TURN_BUFFERS))
             angles = []
             for e in range(2):
                 col = P * (first + e)
@@ -225,9 +226,6 @@ def tile_list_block_bid_features_kernel(
         def gain_on_gpsimd(dst, src, factor):
             nc.gpsimd.tensor_scalar(dst, src, factor, 0.0, ALU.mult, ALU.add)
 
-        def copy_on_gpsimd(out, in_):
-            nc.gpsimd.tensor_scalar(out, in_, 1.0, 0.0, ALU.mult, ALU.add)
-
         def gain_on_scalar(dst, src, factor):
             nc.scalar.activation(dst, src, ACT.Copy, scale=factor)
 
@@ -237,9 +235,19 @@ def tile_list_block_bid_features_kernel(
                 apply_gain(rounded[:, t, :], values[:, t, :], gain_sb[:, b, t : t + 1])
             return rounded
 
-        def group_z(rounded, copy):
-            grouped = ring.tile([P, 4 * W], BF16, name="z_grouped", bufs=2, align_bytes=64)
-            return interleave(grouped, rounded, copy)
+        def z_staging():
+            return ring.tile([P, 4 * W], BF16, name="z_grouped", bufs=2, align_bytes=64)
+
+        def group_z_on_scalar(rounded):
+            return interleave(z_staging(), rounded)
+
+        def group_z_on_gpsimd(rounded):
+            grouped = z_staging()
+            nc.gpsimd.tensor_scalar(
+                grouped[:].rearrange("p (c j) -> p c j", j=4), rounded[:].rearrange("p j c -> p c j"),
+                1.0, 0.0, ALU.mult, ALU.add,
+            )
+            return grouped
 
         def z_codes():
             return ring.tile([P, W], U32, name="z_codes", bufs=4, align_bytes=64)
@@ -268,11 +276,11 @@ def tile_list_block_bid_features_kernel(
             next_cosine = cosine_of(step + 1) if step + 1 < STEPS else None
             if step in Z1_STEPS:
                 b = len(grouped_first)
-                grouped_first.append(group_z(with_gain(tanh_of(0, b), b, gain_on_gpsimd), nc.scalar.copy))
+                grouped_first.append(group_z_on_gpsimd(with_gain(tanh_of(0, b), b, gain_on_gpsimd)))
             h1_of(step, cosine)
             cosine = next_cosine
 
-        last_buffer = "turns%d" % ((STEPS - 1) % 4)
+        last_buffer = "turns%d" % ((STEPS - 1) % TURN_BUFFERS)
         z1_first = [
             quantise_z(grouped_first[0], z_codes()),
             quantise_z(grouped_first[1], keep("held_codes", [P, W], U32, last_buffer)),
@@ -293,7 +301,7 @@ def tile_list_block_bid_features_kernel(
         def w5_of(a):
             rows = ring.tile([P, 4, W], F32, name="w5_rows", tag="tanh", bufs=2)
             nc.sync.dma_start(out=rows[:], in_=w5[W * a : W * (a + 1), :].rearrange("(p j) c -> p j c", j=4))
-            return quantise_weight("w5_%d" % a, interleave(weight_staging(), rows, nc.scalar.copy))
+            return quantise_weight("w5_%d" % a, interleave(weight_staging(), rows))
 
         def peaks_of(b):
             picked = keep("peaks", [P, 4, W], F32, slab(6 + b))
@@ -316,12 +324,12 @@ def tile_list_block_bid_features_kernel(
         for i in range(2):
             place_y1(z1_first, 0, i)
         rounded = with_gain(tanh_of(1, 0), 0, gain_on_scalar)
-        tanh = tanh_of(1, 1)
-        z1_second = [quantise_z(group_z(rounded, nc.scalar.copy), z_codes())]
+        last_tanh = tanh_of(1, 1)
+        z1_second = [quantise_z(group_z_on_scalar(rounded), z_codes())]
         place_y1(z1_first, 0, 2)
-        rounded = with_gain(tanh, 1, gain_on_scalar)
+        rounded = with_gain(last_tanh, 1, gain_on_scalar)
         w3_first = w3_of(0)
-        z1_second.append(quantise_z(group_z(rounded, nc.scalar.copy), z_codes()))
+        z1_second.append(quantise_z(group_z_on_scalar(rounded), z_codes()))
         place_y1(z1_first, 0, 3)
         place_y1(z1_second, 1, 0)
         meet_peaks(0, w3_first)
@@ -332,7 +340,7 @@ def tile_list_block_bid_features_kernel(
         for b in range(2):
             rounded = with_gain(peaks[b], b, gain_on_scalar)
             w5_q.append(w5_of(b))
-            z2.append(quantise_z(group_z(rounded, nc.scalar.copy), z_codes()))
+            z2.append(quantise_z(group_z_on_scalar(rounded), z_codes()))
             place_y1(z1_second, 1, 2 + b)
         for i in range(4):
             place_y2(z2, w5_q, i)

import math
from contextlib import ExitStack

import concourse.mybir as mybir

K, K2, H, N, S, BIDS, SLOTS = 512, 1024, 1024, 512, 1024, 512, 2048
FLOPS = 2 * (2 * K * H * S + K2 * H * BIDS + H * N * S + H * N * BIDS + K2 * N * BIDS)

F32 = mybir.dt.float32
BF16 = mybir.dt.bfloat16
I32 = mybir.dt.int32
U32 = mybir.dt.uint32
U16 = mybir.dt.uint16
U8 = mybir.dt.uint8
E4M3 = mybir.dt.float8_e4m3fn_x4
E2M1 = mybir.dt.float4_e2m1fn_x4
ALU = mybir.AluOpType
ACT = mybir.ActivationFunctionType

P = 128
W = 512
LIST_COLS = W // 16
PER_TURN = 1.0 / (2.0 * math.pi)
Z1_STEPS = (4, 6)
TURN_BUFFERS = 4
STEPS = 8


def tile_list_block_bid_features_kernel(
    tc, tab_words, tab_scales, tab2_words, tab2_scales, offs, offs2, pos1, offs3, offs4,
    w1, w2_words, w2_scales, w3, gain, w4_words, w4_scales, w5, w6_words, w6_scales,
    page1, wg1, wg2, out,
):
    nc = tc.nc
    with ExitStack() as ctx:
        held = ctx.enter_context(tc.tile_pool(name="held", bufs=1))
        ring = ctx.enter_context(tc.tile_pool(name="ring", bufs=2))
        psum = ctx.enter_context(tc.psum_pool(name="psum", bufs=1))

        def keep(name, shape, dtype, buffer=None):
            return held.tile(shape, dtype, name=name, tag=buffer or name, align_bytes=64)

        def slab(n):
            return "slab%d" % n

        def load(name, shape, dtype, src, buffer=None):
            dst = keep(name, shape, dtype, buffer)
            nc.sync.dma_start(out=dst[:], in_=src)
            return dst

        def load_list(name, src):
            lst = held.tile(list(src.shape), U16, name=name)
            nc.sync.dma_start(lst[:], src)
            return lst

        def load_words(name, words, buffer=None):
            flat = words.rearrange("p c i -> p (c i)").bitcast(I32)
            return load(name, list(flat.shape), I32, flat, buffer)

        def load_rows(w, a, cols, buffer):
            rows = w[W * a : W * (a + 1), cols].rearrange("(p j) c -> p j c", j=4)
            return load("rows", [P, 4, W], F32, rows, buffer)

        def load_repeated_scales(name, scales):
            plane = keep(name, [P, scales.shape[1]], U8)
            for q in range(4):
                nc.sync.dma_start(
                    out=plane[32 * q : 32 * (q + 1), :].bitcast(I32),
                    in_=scales[4 * q : 4 * q + 4, :].bitcast(I32).partition_broadcast(8),
                )
            return plane

        def load_stacked_scales(name, scales):
            plane = keep(name, [P, scales.shape[2]], U8)
            nc.gpsimd.memset(plane[:].bitcast(I32), 0)
            for q in range(4):
                nc.sync.dma_start(
                    out=plane[32 * q : 32 * q + 8, :].bitcast(I32),
                    in_=scales[:, 4 * q : 4 * q + 4, :].bitcast(I32),
                )
            return plane

        def load_adjacent_scales(name, scales):
            plane = keep(name, [P, 2, scales.shape[2]], U8)
            nc.gpsimd.memset(plane[:].bitcast(I32), 0)
            for q in range(4):
                nc.sync.dma_start(
                    out=plane[32 * q : 32 * q + 4, :, :].bitcast(I32),
                    in_=scales[:, 4 * q : 4 * q + 4, :].rearrange("a r n -> r a n").bitcast(I32),
                )
            return plane

        def weight_staging():
            return ring.tile([P, 4 * W], BF16, name="w_grouped", bufs=3, align_bytes=64)

        def round_dealt(rows, copy):
            grouped = weight_staging()
            copy(
                out=grouped[:].rearrange("p (t m j) -> p m j t", t=4, j=4),
                in_=rows[:].rearrange("p j (m t) -> p m j t", t=4),
            )
            return grouped

        def interleave(grouped, rows):
            nc.scalar.copy(
                out=grouped[:].rearrange("p (c i j) -> p c j i", i=4, j=4),
                in_=rows[:].rearrange("p j (c i) -> p c j i", i=4),
            )
            return grouped

        def quantise(grouped, codes, scales):
            nc.vector.quantize_mx(out=codes[:].bitcast(E4M3), scales=scales[:], in_=grouped[:])
            return codes, scales

        def quantise_weight(name, grouped):
            return quantise(grouped, keep(name + "_codes", [P, W], U32), keep(name + "_scales", [P, W], U8))

        def multiply(acc, passes):
            for n, (lhs_words, lhs_scales, rhs_words, rhs_scales) in enumerate(passes):
                nc.tensor.matmul_mx(
                    out=acc[:], lhsT=lhs_words, lhsT_scale=lhs_scales, rhs=rhs_words, rhs_scale=rhs_scales,
                    start=(n == 0), stop=(n == len(passes) - 1),
                )
            return acc

        def scalar_bank():
            return psum.tile([P, W], F32, name="scalar_bank", bufs=5)

        def vector_bank():
            return psum.tile([P, W], F32, name="vector_bank", bufs=3)

        def stationary(quantised, n):
            cols = slice(P * n, P * (n + 1))
            return quantised[0][:, cols].bitcast(E4M3), quantised[1][:, cols]

        warm = keep("warm", [P, 1], F32)
        nc.vector.memset(warm[:], 0.0)
        nc.scalar.activation(warm[:], warm[:], ACT.Silu)

        idx = load_list("idx", offs)
        tab_s = load_repeated_scales("tab_s", tab_scales[0])
        w2_w = load("w2_w", [P, H // 2], I32, w2_words[0].bitcast(I32))
        tab_w = load_words("tab_w", tab_words[0], slab(0))
        w2_s = load_repeated_scales("w2_s", w2_scales[0])
        w1_rows = [load_rows(w1, 0, slice(W * b, W * (b + 1)), slab(1 + b)) for b in range(2)]
        gain_sb = load("gain_sb", [P, 2, 4], F32, gain.rearrange("(b p t) -> p b t", b=2, t=4))
        idx2 = load_list("idx2", offs2)
        peak_idx = load_list("peak_idx", pos1)
        idx3 = load_list("idx3", offs3)
        idx4 = load_list("idx4", offs4)
        tab2_s = load_stacked_scales("tab2_s", tab2_scales)
        tab2_w = [load_words("tab2_w%d" % a, tab2_words[a], slab(6 + a)) for a in range(2)]
        w4_w = [load("w4_w%d" % a, [P, N // 2], I32, w4_words[a].bitcast(I32)) for a in range(2)]
        w4_s = load_adjacent_scales("w4_s", w4_scales)
        wg1_sb = load("wg1_sb", [P, S], F32, wg1)

        def load_page(i):
            return load("page%d" % i, [P, SLOTS], F32, page1[P * i : P * (i + 1), :], slab(i))

        pages = [load_page(i) for i in range(2)]
        w3_rows = [load_rows(w3, a, slice(0, W), slab(4 + a)) for a in range(2)]
        pages.extend([load_page(i) for i in range(2, 4)])
        w6_s = load_stacked_scales("w6_s", w6_scales)
        w6_w = [load_words("w6_w%d" % a, w6_words[a]) for a in range(2)]
        wg2_sb = load("wg2_sb", [P, BIDS], F32, wg2)

        w2d_w = keep("w2d_w", [P, 2 * H], U8)
        w2d_s = keep("w2d_s", [P, H], U8)
        nc.vector.tensor_copy(
            out=w2d_w[:].bitcast(U16).rearrange("p (b t m) -> p b m t", b=2, t=4),
            in_=w2_w[:].bitcast(U16).rearrange("p (b m t) -> p b m t", b=2, t=4),
        )
        nc.vector.tensor_copy(
            out=w2d_s[:].rearrange("p (b t m) -> p b m t", b=2, t=4),
            in_=w2_s[:].rearrange("p (b m t) -> p b m t", b=2, t=4),
        )

        def hours_of(c, buffer):
            entries = idx[:, LIST_COLS * c : LIST_COLS * (c + 1)]
            words = keep("v_w%d" % c, [P, W], U32, buffer)
            scales = keep("v_s%d" % c, [P, W], U8)
            nc.vector.tensor_copy(words[:], tab_w[:].bitcast(U32).indirect(entries))
            nc.vector.tensor_copy(scales[:], tab_s[:].indirect(entries))
            return words[:].bitcast(E4M3), scales[:]

        hours = [hours_of(0, None)]
        w1_q = [
            quantise_weight("w1_%d" % b, round_dealt(w1_rows[b], copy))
            for b, copy in enumerate((nc.vector.tensor_copy, nc.scalar.copy))
        ]
        hours.append(hours_of(1, "w2_s"))

        h1 = [keep("h1_%d" % b, [P, 4, S], F32) for b in range(2)]

        def cosine_of(step):
            c, first = step // 4, 2 * (step % 4)
            turns = keep("turns", [P, 2, W], F32, "turns%d" % (step % TURN_BUFFERS))
            angles = []
            for e in range(2):
                col = P * (first + e)
                w2_pass = (w2d_w[:, 2 * col : 2 * (col + P)].bitcast(E2M1), w2d_s[:, col : col + P])
                angles.append(multiply(scalar_bank(), [w2_pass + hours[c]]))
                nc.scalar.activation(turns[:, e, :], angles[e][:], ACT.Copy, scale=PER_TURN)
            whole = ring.tile([P, 2, W], I32, name="whole", bufs=2)
            nc.gpsimd.tensor_scalar(whole[:], turns[:], 1.0, 0.25, ALU.mult, ALU.add)
            for e in range(2):
                nc.vector.scalar_tensor_tensor(
                    turns[:, e, :], angles[e][:], PER_TURN, whole[:, e, :], ALU.mult, ALU.subtract
                )
            nc.scalar.activation(turns[:], turns[:], ACT.Sin, scale=2.0 * math.pi, bias=0.5 * math.pi)
            return turns

        def h1_of(step, cosine):
            c, b, first = step // 4, step // 2 % 2, 2 * (step % 2)
            for e in range(2):
                acc = multiply(vector_bank(), [stationary(w1_q[b], first + e) + hours[c]])
                nc.vector.tensor_tensor(
                    h1[b][:, first + e, W * c : W * (c + 1)], acc[:], cosine[:, e, :], ALU.add
                )

        def tanh_of(c, b):
            tanh = ring.tile([P, 4, W], F32, name="tanh", bufs=2)
            nc.scalar.activation(tanh[:], h1[b][:, :, W * c : W * (c + 1)], ACT.Tanh)
            return tanh

        def gain_on_gpsimd(dst, src, factor):
            nc.gpsimd.tensor_scalar(dst, src, factor, 0.0, ALU.mult, ALU.add)

        def gain_on_scalar(dst, src, factor):
            nc.scalar.activation(dst, src, ACT.Copy, scale=factor)

        def with_gain(values, b, apply_gain):
            rounded = ring.tile([P, 4, W], BF16, name="rounded", bufs=2)
            for t in range(4):
                apply_gain(rounded[:, t, :], values[:, t, :], gain_sb[:, b, t : t + 1])
            return rounded

        def z_staging():
            return ring.tile([P, 4 * W], BF16, name="z_grouped", bufs=2, align_bytes=64)

        def group_z_on_scalar(rounded):
            return interleave(z_staging(), rounded)

        def group_z_on_gpsimd(rounded):
            grouped = z_staging()
            nc.gpsimd.tensor_scalar(
                grouped[:].rearrange("p (c j) -> p c j", j=4), rounded[:].rearrange("p j c -> p c j"),
                1.0, 0.0, ALU.mult, ALU.add,
            )
            return grouped

        def z_codes():
            return ring.tile([P, W], U32, name="z_codes", bufs=4, align_bytes=64)

        def quantise_z(grouped, codes):
            scales = ring.tile([P, W], U8, name="z_scales", bufs=4, align_bytes=64)
            quantise(grouped, codes, scales)
            return codes[:].bitcast(E4M3), scales[:]

        def place(passes, i, entries, factors):
            y = ring.tile([P, W], F32, name="y", bufs=4)
            nc.scalar.copy(out=y[:], in_=multiply(scalar_bank(), passes)[:])
            nc.vector.tensor_tensor(pages[i][:].indirect(entries), y[:], factors, ALU.mult)

        def place_y1(z1, c, i):
            passes = [
                (w4_w[a][:].bitcast(U8)[:, 2 * P * i : 2 * P * (i + 1)].bitcast(E2M1), w4_s[:, a, P * i : P * (i + 1)])
                + z1[a]
                for a in range(2)
            ]
            place(passes, i, idx3[:, LIST_COLS * c : LIST_COLS * (c + 1)], wg1_sb[:, W * c : W * (c + 1)])

        grouped_first = []
        cosine = cosine_of(0)
        for step in range(STEPS):
            next_cosine = cosine_of(step + 1) if step + 1 < STEPS else None
            if step in Z1_STEPS:
                b = len(grouped_first)
                grouped_first.append(group_z_on_gpsimd(with_gain(tanh_of(0, b), b, gain_on_gpsimd)))
            h1_of(step, cosine)
            cosine = next_cosine

        last_buffer = "turns%d" % ((STEPS - 1) % TURN_BUFFERS)
        z1_first = [
            quantise_z(grouped_first[0], z_codes()),
            quantise_z(grouped_first[1], keep("held_codes", [P, W], U32, last_buffer)),
        ]

        v2_s = keep("v2_s", [P, BIDS], U8)
        bids = []
        for a in range(2):
            words = keep("v2_w%d" % a, [P, BIDS], U32)
            nc.vector.tensor_copy(words[:], tab2_w[a][:].bitcast(U32).indirect(idx2[:]))
            bids.append((words[:].bitcast(E4M3), v2_s[4 * a : P, :]))
        nc.vector.tensor_copy(v2_s[:], tab2_s[:].indirect(idx2[:]))

        def w3_of(b):
            rows = w3_rows if b == 0 else [load_rows(w3, a, slice(W, 2 * W), "h1_%d" % a) for a in range(2)]
            return [quantise_weight("w3_%d_%d" % (a, b), round_dealt(rows[a], nc.scalar.copy)) for a in range(2)]

        def w5_of(a):
            rows = ring.tile([P, 4, W], F32, name="w5_rows", tag="tanh", bufs=2)
            nc.sync.dma_start(out=rows[:], in_=w5[W * a : W * (a + 1), :].rearrange("(p j) c -> p j c", j=4))
            return quantise_weight("w5_%d" % a, interleave(weight_staging(), rows))

        def peaks_of(b):
            picked = keep("peaks", [P, 4, W], F32, slab(6 + b))
            for t in range(4):
                nc.vector.tensor_copy(picked[:, t, :], h1[b][:, t, :].indirect(peak_idx[:]))
            return picked

        def meet_peaks(b, w3_q):
            for t in range(4):
                acc = multiply(vector_bank(), [stationary(w3_q[a], t) + bids[a] for a in range(2)])
                nc.vector.tensor_tensor(peaks[b][:, t, :], acc[:], peaks[b][:, t, :], ALU.max)

        def place_y2(z2, w5_q, i):
            cols = slice(P * i, P * (i + 1))
            passes = [(w6_w[a][:, cols].bitcast(E4M3), w6_s[4 * a : P, cols]) + bids[a] for a in range(2)]
            passes.extend([stationary(w5_q[a], i) + z2[a] for a in range(2)])
            place(passes, i, idx4[:], wg2_sb[:])

        peaks = [peaks_of(b) for b in range(2)]
        for i in range(2):
            place_y1(z1_first, 0, i)
        rounded = with_gain(tanh_of(1, 0), 0, gain_on_scalar)
        last_tanh = tanh_of(1, 1)
        z1_second = [quantise_z(group_z_on_scalar(rounded), z_codes())]
        place_y1(z1_first, 0, 2)
        rounded = with_gain(last_tanh, 1, gain_on_scalar)
        w3_first = w3_of(0)
        z1_second.append(quantise_z(group_z_on_scalar(rounded), z_codes()))
        place_y1(z1_first, 0, 3)
        place_y1(z1_second, 1, 0)
        meet_peaks(0, w3_first)
        w3_second = w3_of(1)
        place_y1(z1_second, 1, 1)
        meet_peaks(1, w3_second)
        z2, w5_q = [], []
        for b in range(2):
            rounded = with_gain(peaks[b], b, gain_on_scalar)
            w5_q.append(w5_of(b))
            z2.append(quantise_z(group_z_on_scalar(rounded), z_codes()))
            place_y1(z1_second, 1, 2 + b)
        for i in range(4):
            place_y2(z2, w5_q, i)
            nc.sync.dma_start(out=out[P * i : P * (i + 1), :], in_=pages[i][:])
